import numpy as np
import ml_dtypes


def mxq(x, axis, fmt="e4m3"):
    dtype, down = {"e4m3": (ml_dtypes.float8_e4m3fn, 7), "e5m2": (ml_dtypes.float8_e5m2, 14)}[fmt]
    v = np.moveaxis(np.asarray(x, np.float32).astype(ml_dtypes.bfloat16).astype(np.float64), axis, -1)
    blocks = v.reshape(v.shape[:-1] + (-1, 32))
    amax = np.abs(blocks).max(-1, keepdims=True)
    byte = np.maximum(np.where(amax > 0, np.frexp(amax)[1] - 1 + 127, 0) - down, 1)
    scale = np.exp2(byte - 127.0)
    codes = (blocks / scale).astype(np.float32).astype(dtype).astype(np.float64)
    return np.moveaxis((codes * scale).reshape(v.shape), -1, axis)


WIDE = False


def mx_kscale(k):
    if not WIDE:
        return np.ones(k)
    levels = np.array([10, -10, 5, -5, 0])
    if k % 512:
        return np.exp2(np.random.permutation(np.resize(levels, k // 32))).repeat(32)
    a = np.empty((k // 512, 16))
    for p in range(k // 512):
        a[p, :8] = np.random.permutation(np.resize(levels, 8))
        for g in range(8):
            far = levels[np.abs(levels - a[p, g]) >= 10]
            a[p, g + 8] = far[np.random.randint(len(far))]
    return np.exp2(a.ravel()).repeat(32)


def f64(x):
    return np.asarray(x).astype(np.float64)


def striped(idx):
    return np.tile(idx.reshape(-1, 16).T, (8, 1)).astype(np.uint16)


def unstriped(offs):
    return offs[:16].T.reshape(-1).astype(np.int64)


def pack_weight(w):
    k, n = w.shape
    w = f64(np.asarray(w, np.float32).astype(ml_dtypes.bfloat16)).reshape(k // 32, 32, n)
    amax = np.abs(w).max(1)
    byte = np.clip(np.where(amax > 0, np.frexp(amax)[1] - 1 + 127 - 7, 1), 1, 254)
    scaled = (w * np.exp2(127.0 - byte)[:, None, :]).reshape(k, n).astype(np.float32)
    words = np.ascontiguousarray(scaled.reshape(k // 512, 128, 4, n).transpose(0, 1, 3, 2)).astype(ml_dtypes.float8_e4m3fn).view(np.uint8)
    return words, np.ascontiguousarray(byte.astype(np.uint8).reshape(k // 512, 16, n))


def unpack_weight(words, scales):
    g, p, n, _ = words.shape
    vals = np.ascontiguousarray(words).view(ml_dtypes.float8_e4m3fn).astype(np.float64) * np.repeat(np.exp2(scales.astype(np.float64) - 127.0), 8, axis=1)[..., None]
    return vals.transpose(0, 1, 3, 2).reshape(g * 512, n)


K, T, S, N = 1024, 2048, 512, 128
P = 2 ** 7


def setup_inputs():
    n = np.random.standard_normal
    s = mx_kscale(K)[:, None]
    packed_xT = pack_weight(n((K, T)) * s)
    return {
        "x_words": packed_xT[0],
        "x_scales": packed_xT[1],
        "w1": (n((K, N)) / np.sqrt(K) / s).astype(np.float32),
        "w2": (n((K, N)) / np.sqrt(K) / s).astype(np.float32),
        "mat": (n((N, S))).astype(np.float32),
        "ins": (n((N, S)) - 0.5).astype(np.float32),
        "tmm": (np.tile(-np.random.uniform(0.0, 0.5, S), (P, 1))).astype(np.float32),
        "gop": (np.tile(-np.random.uniform(0.5, 1.5, S), (P, 1))).astype(np.float32),
        "ext": (np.random.uniform(0.3, 1.5, (N, 1))).astype(np.float32),
        "offs": striped(np.random.permutation(T)[:S]),
    }


def reference(x_words, x_scales, w1, w2, mat, ins, tmm, gop, ext, offs):
    xq = unpack_weight(x_words, x_scales)[:, unstriped(offs)]
    ym = mxq(f64(w1), 0, "e4m3").T @ xq
    mnew = ym + np.maximum(np.pad(f64(mat), ((0, 0), (1, 0)))[:, :S] + f64(tmm)[:1], np.pad(f64(ins), ((0, 0), (1, 0)))[:, :S] + 0.5 * f64(gop)[:1])
    yi = mxq(f64(w2), 0, "e4m3").T @ xq
    inew = 0.5 * yi + np.maximum(f64(mat) + f64(gop)[:1], f64(ins) + f64(ext) * f64(tmm)[:1])
    dela = np.pad(mnew, ((0, 0), (1, 0)))[:, :S] + f64(gop)[:1]
    delb = np.maximum(dela, np.pad(dela, ((0, 0), (1, 0)))[:, :S] - 0.4)
    return np.maximum(np.maximum(mnew, inew), delb)

@@ -1,0 +1,196 @@
+from contextlib import ExitStack
+
+import concourse.mybir as mybir
+from concourse.masks import make_identity
+
+K, T, S, N = 1024, 2048, 512, 128
+P = 128
+PACK = 4
+K_PASS = P * PACK
+PASSES = K // K_PASS
+HALF = S // 2
+PAD = 8
+QUADS = 4
+QUAD = P // QUADS
+ROWS = 4
+FLOPS = 2 * 2 * K * N * S
+
+F32 = mybir.dt.float32
+BF16 = mybir.dt.bfloat16
+I32 = mybir.dt.int32
+U32 = mybir.dt.uint32
+U16 = mybir.dt.uint16
+U8 = mybir.dt.uint8
+FP8X4 = mybir.dt.float8_e4m3fn_x4
+ADD = mybir.AluOpType.add
+MULT = mybir.AluOpType.mult
+MAX = mybir.AluOpType.max
+
+
+def tile_picked_yvitph_best_p_kernel(
+    tc, x_words, x_scales, w1, w2, mat, ins, tmm, gop, ext, offs, out
+):
+    nc = tc.nc
+    with ExitStack() as ctx:
+        sb = ctx.enter_context(tc.tile_pool(name="sb", bufs=1))
+        ps = ctx.enter_context(tc.psum_pool(name="ps", bufs=1))
+
+        offsets = sb.tile([P, S // 16], U16, name="offsets")
+        scale_table = sb.tile([P, T], U8, name="scale_table", align_bytes=64)
+        word_table = [sb.tile([P, T], U32, name=f"word_table{o}", align_bytes=64) for o in range(PASSES)]
+        picked_rows = sb.tile([P, S], U8, name="picked_rows", align_bytes=64)
+        x_planes = sb.tile([P, PASSES, S], U8, name="x_planes", align_bytes=64)
+        x_codes = [sb.tile([P, S], U32, name=f"x_codes{o}", align_bytes=64) for o in range(PASSES)]
+        tmm_cols = sb.tile([P, PACK], F32, name="tmm_cols")
+        gop_cols = sb.tile([P, PACK], F32, name="gop_cols")
+        ext_col = sb.tile([P, 1], F32, name="ext_col")
+        ident = sb.tile([P, P], F32, name="ident")
+        padded = sb.tile([P, 4, PAD + S], F32, name="padded")
+        mat_p, ins_p, mnew_p, dela_p = (padded[:, i, :] for i in range(4))
+
+        def here(t, lo=0, hi=S):
+            return t[:, PAD + lo : PAD + hi]
+
+        def before(t, lo=0, hi=S):
+            return t[:, PAD - 1 + lo : PAD - 1 + hi]
+
+        def by4(ap):
+            return ap.rearrange("p (n c) -> p n c", c=PACK)
+
+        w1_raw = sb.tile([P, PASSES, PACK, N], F32, name="w1_raw")
+        w2_raw = [sb.tile([P, PACK, N], F32, name=f"w2_raw{o}") for o in range(PASSES)]
+
+        n_rows = PASSES * QUADS * ROWS
+        top = P - n_rows
+        nc.sync.dma_start(offsets[:], offs)
+        nc.sync.dma_start(
+            scale_table[top:, :].bitcast(I32), x_scales.rearrange("o r c -> r o c").bitcast(I32)
+        )
+        nc.scalar.dma_start(tmm_cols[:], tmm[0].rearrange("(n c) -> n c", c=PACK))
+        nc.scalar.dma_start(gop_cols[:], gop[0].rearrange("(n c) -> n c", c=PACK))
+        nc.sync.dma_start(here(mat_p), mat)
+        nc.sync.dma_start(here(ins_p), ins)
+
+        def load_words(o):
+            nc.sync.dma_start(
+                word_table[o][:].bitcast(I32), x_words[o].rearrange("p n t -> p (n t)").bitcast(I32)
+            )
+
+        load_words(0)
+        nc.sync.dma_start(w1_raw[:], w1.rearrange("(o p j) m -> p o j m", o=PASSES, j=PACK))
+        load_words(1)
+        for o in range(PASSES):
+            nc.sync.dma_start(
+                w2_raw[o][:], w2[o * K_PASS : (o + 1) * K_PASS, :].rearrange("(p j) m -> p j m", j=PACK)
+            )
+
+        nc.vector.memset(scale_table[:top, :].bitcast(I32), 0)
+        make_identity(nc, ident[:])
+        nc.vector.memset(padded[:, :, :PAD], 0.0)
+        nc.vector.memset(x_planes[:].rearrange("p o s -> p (o s)").bitcast(I32), 0)
+        nc.gpsimd.dma_start(ext_col[:], ext)
+
+        tmm_ps = ps.tile([P, PACK, P], F32, name="tmm_ps")
+        gop_ps = ps.tile([P, PACK, P], F32, name="gop_ps")
+        for cols, bank in ((tmm_cols, tmm_ps), (gop_cols, gop_ps)):
+            for c in range(PACK):
+                nc.tensor.transpose(bank[:, c, :], cols[:, c : c + 1].to_broadcast([P, P]), ident[:])
+
+        def row(bank, lo=0, hi=S):
+            return bank[:].rearrange("p c n -> p n c")[:, lo // PACK : hi // PACK, :]
+
+        nc.vector.tensor_copy(picked_rows[:], scale_table[:].indirect(offsets[:]))
+        per_quad = PASSES * ROWS
+        for q in range(QUADS):
+            nc.scalar.dma_start(
+                x_planes[QUAD * q : QUAD * q + ROWS].rearrange("p o s -> p (o s)").bitcast(I32),
+                picked_rows[top + per_quad * q : top + per_quad * (q + 1), :].bitcast(I32),
+            )
+
+        s1 = sb.tile([P, S], F32, name="s1")
+        s2 = sb.tile([P, S], F32, name="s2")
+        s3 = sb.tile([P, S], F32, name="s3")
+        s4 = sb.tile([P, S], F32, name="s4")
+        into_match = sb.tile([P, S], F32, name="into_match")
+        into_insert = sb.tile([P, S], F32, name="into_insert")
+        nc.vector.tensor_tensor(by4(s1[:]), row(tmm_ps), by4(before(mat_p)), ADD)
+        nc.vector.scalar_tensor_tensor(by4(s2[:]), row(gop_ps), 0.5, by4(before(ins_p)), MULT, ADD)
+        nc.vector.tensor_tensor(by4(s3[:]), row(gop_ps), by4(here(mat_p)), ADD)
+        nc.vector.scalar_tensor_tensor(by4(s4[:]), row(tmm_ps), ext_col[:], by4(here(ins_p)), MULT, ADD)
+        nc.vector.tensor_copy(x_codes[0][:], word_table[0][:].indirect(offsets[:]))
+        nc.vector.tensor_tensor(into_match[:], s1[:], s2[:], MAX)
+        nc.vector.tensor_tensor(into_insert[:], s3[:], s4[:], MAX)
+
+        def weave(raw, name):
+            woven = sb.tile([P, N, PACK], BF16, name=name, align_bytes=64)
+            nc.scalar.copy(
+                woven[:].rearrange("p (c i) j -> p c j i", i=4), raw.rearrange("p j (c i) -> p c j i", i=4)
+            )
+            return woven
+
+        def quantize(woven, name):
+            codes = sb.tile([P, N], U32, name=name + "_codes", align_bytes=64)
+            plane = sb.tile([P, N], U8, name=name + "_plane", align_bytes=64)
+            nc.vector.quantize_mx(
+                out=codes[:].bitcast(FP8X4), scales=plane[:], in_=woven[:].rearrange("p m j -> p (m j)")
+            )
+            return codes, plane
+
+        def product(bank, weights, o, h):
+            codes, plane = weights
+            cols = slice(h * HALF, (h + 1) * HALF)
+            nc.tensor.matmul_mx(
+                out=bank[:],
+                lhsT=codes[:].bitcast(FP8X4),
+                lhsT_scale=plane[:],
+                rhs=x_codes[o][:, cols].bitcast(FP8X4),
+                rhs_scale=x_planes[:, o, cols],
+                start=(o == 0),
+                stop=(o == PASSES - 1),
+            )
+
+        ym = [ps.tile([P, HALF], F32, name=f"ym{h}") for h in range(2)]
+        yi = [ps.tile([P, HALF], F32, name=f"yi{h}") for h in range(2)]
+
+        w1_woven = [weave(w1_raw[:, o], f"w1_woven{o}") for o in range(PASSES)]
+        w1_q = [quantize(w1_woven[o], f"w1_{o}") for o in range(PASSES)]
+        for h in range(2):
+            product(ym[h], w1_q[0], 0, h)
+        per_half = HALF // 16
+        for h in range(2):
+            nc.vector.tensor_copy(
+                x_codes[1][:, h * HALF : (h + 1) * HALF],
+                word_table[1][:].indirect(offsets[:, h * per_half : (h + 1) * per_half]),
+            )
+            product(ym[h], w1_q[1], 1, h)
+
+        w2_woven = [weave(w2_raw[o][:], f"w2_woven{o}") for o in range(PASSES)]
+        halves = [(h, h * HALF, (h + 1) * HALF) for h in range(2)]
+        delb = sb.tile([P, S], F32, name="delb")
+        best = sb.tile([P, S], F32, name="best")
+        inew = sb.tile([P, S], F32, name="inew")
+        result = sb.tile([P, S], F32, name="result")
+        for h, lo, hi in halves:
+            nc.vector.tensor_tensor(here(mnew_p, lo, hi), ym[h][:], into_match[:, lo:hi], ADD)
+        w2_q0 = quantize(w2_woven[0], "w2_0")
+        for h in range(2):
+            product(yi[h], w2_q0, 0, h)
+        for h, lo, hi in halves:
+            nc.vector.tensor_tensor(
+                by4(here(dela_p, lo, hi)), row(gop_ps, lo, hi), by4(before(mnew_p, lo, hi)), ADD
+            )
+        w2_q1 = quantize(w2_woven[1], "w2_1")
+        for h in range(2):
+            product(yi[h], w2_q1, 1, h)
+        for h, lo, hi in halves:
+            nc.vector.scalar_tensor_tensor(
+                delb[:, lo:hi], before(dela_p, lo, hi), -0.4, here(dela_p, lo, hi), ADD, MAX
+            )
+        for h, lo, hi in halves:
+            nc.vector.tensor_tensor(best[:, lo:hi], here(mnew_p, lo, hi), delb[:, lo:hi], MAX)
+        for h, lo, hi in halves:
+            nc.vector.scalar_tensor_tensor(inew[:, lo:hi], yi[h][:], 0.5, into_insert[:, lo:hi], MULT, ADD)
+        for h, lo, hi in halves:
+            nc.vector.tensor_tensor(result[:, lo:hi], best[:, lo:hi], inew[:, lo:hi], MAX)
+            queue = nc.sync if h == 0 else nc.scalar
+            queue.dma_start(out[:, lo:hi], result[:, lo:hi])

@@ -25,6 +25,7 @@ FP8X4 = mybir.dt.float8_e4m3fn_x4
 ADD = mybir.AluOpType.add
 MULT = mybir.AluOpType.mult
 MAX = mybir.AluOpType.max
+COPY = mybir.ActivationFunctionType.Copy
 
 
 def tile_picked_yvitph_best_p_kernel(
@@ -36,17 +37,23 @@ def tile_picked_yvitph_best_p_kernel(
         ps = ctx.enter_context(tc.psum_pool(name="ps", bufs=1))
 
         offsets = sb.tile([P, S // 16], U16, name="offsets")
-        scale_table = sb.tile([P, T], U8, name="scale_table", align_bytes=64)
-        word_table = [sb.tile([P, T], U32, name=f"word_table{o}", align_bytes=64) for o in range(PASSES)]
+        late = ctx.enter_context(tc.tile_pool(name="late", bufs=1))
+        w2_bytes = PASSES * PACK * N * 4
+        scale_table = late.tile([P, T], U8, name="scale_table", align_bytes=64, offset=w2_bytes - 64)
+        word_table = [
+            sb.tile([P, T], U32, name="word_table0", align_bytes=64),
+            late.tile([P, T], U32, name="word_table1", align_bytes=64, offset=w2_bytes),
+        ]
         picked_rows = sb.tile([P, S], U8, name="picked_rows", align_bytes=64)
         x_planes = sb.tile([P, PASSES, S], U8, name="x_planes", align_bytes=64)
-        x_codes = [sb.tile([P, S], U32, name=f"x_codes{o}", align_bytes=64) for o in range(PASSES)]
         tmm_cols = sb.tile([P, PACK], F32, name="tmm_cols")
         gop_cols = sb.tile([P, PACK], F32, name="gop_cols")
-        ext_col = sb.tile([P, 1], F32, name="ext_col")
+        ext_col = sb.tile([P, 1], F32, name="ext_col", tag="chain", align_bytes=64)
         ident = sb.tile([P, P], F32, name="ident")
-        padded = sb.tile([P, 4, PAD + S], F32, name="padded")
-        mat_p, ins_p, mnew_p, dela_p = (padded[:, i, :] for i in range(4))
+        mat_t = sb.tile([P, PAD + S], F32, name="mat_t", tag="mat", align_bytes=64)
+        mat_p = mat_t[:]
+        padded = sb.tile([P, 3, PAD + S], F32, name="padded")
+        ins_p, mnew_p, dela_p = (padded[:, i, :] for i in range(3))
 
         def here(t, lo=0, hi=S):
             return t[:, PAD + lo : PAD + hi]
@@ -58,7 +65,8 @@ def tile_picked_yvitph_best_p_kernel(
             return ap.rearrange("p (n c) -> p n c", c=PACK)
 
         w1_raw = sb.tile([P, PASSES, PACK, N], F32, name="w1_raw")
-        w2_raw = [sb.tile([P, PACK, N], F32, name=f"w2_raw{o}") for o in range(PASSES)]
+        w2_both = late.tile([P, PASSES, PACK, N], F32, name="w2_both", align_bytes=64, offset=0)
+        w2_raw = [w2_both[:, o] for o in range(PASSES)]
 
         n_rows = PASSES * QUADS * ROWS
         top = P - n_rows
@@ -66,8 +74,9 @@ def tile_picked_yvitph_best_p_kernel(
         nc.sync.dma_start(
             scale_table[top:, :].bitcast(I32), x_scales.rearrange("o r c -> r o c").bitcast(I32)
         )
-        nc.scalar.dma_start(tmm_cols[:], tmm[0].rearrange("(n c) -> n c", c=PACK))
         nc.scalar.dma_start(gop_cols[:], gop[0].rearrange("(n c) -> n c", c=PACK))
+        nc.scalar.dma_start(tmm_cols[:], tmm[0].rearrange("(n c) -> n c", c=PACK))
+        nc.scalar.dma_start(ext_col[:], ext)
         nc.sync.dma_start(here(mat_p), mat)
         nc.sync.dma_start(here(ins_p), ins)
 
@@ -78,21 +87,16 @@ def tile_picked_yvitph_best_p_kernel(
 
         load_words(0)
         nc.sync.dma_start(w1_raw[:], w1.rearrange("(o p j) m -> p o j m", o=PASSES, j=PACK))
-        load_words(1)
-        for o in range(PASSES):
-            nc.sync.dma_start(
-                w2_raw[o][:], w2[o * K_PASS : (o + 1) * K_PASS, :].rearrange("(p j) m -> p j m", j=PACK)
-            )
 
         nc.vector.memset(scale_table[:top, :].bitcast(I32), 0)
         make_identity(nc, ident[:])
         nc.vector.memset(padded[:, :, :PAD], 0.0)
+        nc.vector.memset(mat_t[:, :PAD], 0.0)
         nc.vector.memset(x_planes[:].rearrange("p o s -> p (o s)").bitcast(I32), 0)
-        nc.gpsimd.dma_start(ext_col[:], ext)
 
         tmm_ps = ps.tile([P, PACK, P], F32, name="tmm_ps")
         gop_ps = ps.tile([P, PACK, P], F32, name="gop_ps")
-        for cols, bank in ((tmm_cols, tmm_ps), (gop_cols, gop_ps)):
+        for cols, bank in ((gop_cols, gop_ps), (tmm_cols, tmm_ps)):
             for c in range(PACK):
                 nc.tensor.transpose(bank[:, c, :], cols[:, c : c + 1].to_broadcast([P, P]), ident[:])
 
@@ -102,47 +106,50 @@ def tile_picked_yvitph_best_p_kernel(
         nc.vector.tensor_copy(picked_rows[:], scale_table[:].indirect(offsets[:]))
         per_quad = PASSES * ROWS
         for q in range(QUADS):
-            nc.scalar.dma_start(
+            nc.sync.dma_start(
                 x_planes[QUAD * q : QUAD * q + ROWS].rearrange("p o s -> p (o s)").bitcast(I32),
                 picked_rows[top + per_quad * q : top + per_quad * (q + 1), :].bitcast(I32),
             )
+        load_words(1)
+        for o in range(PASSES):
+            nc.sync.dma_start(
+                w2_raw[o], w2[o * K_PASS : (o + 1) * K_PASS, :].rearrange("(p j) m -> p j m", j=PACK)
+            )
 
         s1 = sb.tile([P, S], F32, name="s1")
-        s2 = sb.tile([P, S], F32, name="s2")
+        s2 = sb.tile([P, S], F32, name="s2", tag="s2", align_bytes=64)
         s3 = sb.tile([P, S], F32, name="s3")
-        s4 = sb.tile([P, S], F32, name="s4")
-        into_match = sb.tile([P, S], F32, name="into_match")
+        s4 = sb.tile([P, S], F32, name="s4", tag="s4", align_bytes=64)
+        into_match = sb.tile([P, S], F32, name="into_match", tag="into_match", align_bytes=64)
         into_insert = sb.tile([P, S], F32, name="into_insert")
         nc.vector.tensor_tensor(by4(s1[:]), row(tmm_ps), by4(before(mat_p)), ADD)
-        nc.vector.scalar_tensor_tensor(by4(s2[:]), row(gop_ps), 0.5, by4(before(ins_p)), MULT, ADD)
+        half_gop = sb.tile([P, S], F32, name="half_gop")
+        ext_tmm = sb.tile([P, S], F32, name="ext_tmm")
+        nc.scalar.activation(by4(half_gop[:]), row(gop_ps), COPY, scale=0.5)
+        nc.scalar.activation(by4(ext_tmm[:]), row(tmm_ps), COPY, scale=ext_col[:])
+        nc.gpsimd.tensor_tensor(s2[:], before(ins_p), half_gop[:], ADD)
+        nc.gpsimd.tensor_tensor(s4[:], here(ins_p), ext_tmm[:], ADD)
         nc.vector.tensor_tensor(by4(s3[:]), row(gop_ps), by4(here(mat_p)), ADD)
-        nc.vector.scalar_tensor_tensor(by4(s4[:]), row(tmm_ps), ext_col[:], by4(here(ins_p)), MULT, ADD)
+        x_codes = [sb.tile([P, S], U32, name="x_codes0", tag="mat", align_bytes=64)]
         nc.vector.tensor_copy(x_codes[0][:], word_table[0][:].indirect(offsets[:]))
         nc.vector.tensor_tensor(into_match[:], s1[:], s2[:], MAX)
         nc.vector.tensor_tensor(into_insert[:], s3[:], s4[:], MAX)
 
-        def weave(raw, name):
-            woven = sb.tile([P, N, PACK], BF16, name=name, align_bytes=64)
+        def weave(woven, raw):
             nc.scalar.copy(
-                woven[:].rearrange("p (c i) j -> p c j i", i=4), raw.rearrange("p j (c i) -> p c j i", i=4)
+                woven.rearrange("p (c i) j -> p c j i", i=4), raw.rearrange("p j (c i) -> p c j i", i=4)
             )
-            return woven
 
-        def quantize(woven, name):
-            codes = sb.tile([P, N], U32, name=name + "_codes", align_bytes=64)
-            plane = sb.tile([P, N], U8, name=name + "_plane", align_bytes=64)
-            nc.vector.quantize_mx(
-                out=codes[:].bitcast(FP8X4), scales=plane[:], in_=woven[:].rearrange("p m j -> p (m j)")
-            )
-            return codes, plane
+        def quantize(codes, plane, woven):
+            nc.vector.quantize_mx(out=codes.bitcast(FP8X4), scales=plane, in_=woven)
 
         def product(bank, weights, o, h):
             codes, plane = weights
             cols = slice(h * HALF, (h + 1) * HALF)
             nc.tensor.matmul_mx(
                 out=bank[:],
-                lhsT=codes[:].bitcast(FP8X4),
-                lhsT_scale=plane[:],
+                lhsT=codes.bitcast(FP8X4),
+                lhsT_scale=plane,
                 rhs=x_codes[o][:, cols].bitcast(FP8X4),
                 rhs_scale=x_planes[:, o, cols],
                 start=(o == 0),
@@ -152,8 +159,14 @@ def tile_picked_yvitph_best_p_kernel(
         ym = [ps.tile([P, HALF], F32, name=f"ym{h}") for h in range(2)]
         yi = [ps.tile([P, HALF], F32, name=f"yi{h}") for h in range(2)]
 
-        w1_woven = [weave(w1_raw[:, o], f"w1_woven{o}") for o in range(PASSES)]
-        w1_q = [quantize(w1_woven[o], f"w1_{o}") for o in range(PASSES)]
+        w1_woven = sb.tile([P, PASSES, N, PACK], BF16, name="w1_woven", tag="chain", align_bytes=64)
+        for o in range(PASSES):
+            weave(w1_woven[:, o], w1_raw[:, o])
+        w1_codes = sb.tile([P, PASSES * N], U32, name="w1_codes", tag="s4", align_bytes=64)
+        w1_plane = sb.tile([P, PASSES * N], U8, name="w1_plane", tag="s2", align_bytes=64)
+        quantize(w1_codes[:], w1_plane[:], w1_woven[:].rearrange("p o m j -> p (o m j)"))
+        w1_q = [(w1_codes[:, o * N : (o + 1) * N], w1_plane[:, o * N : (o + 1) * N]) for o in range(PASSES)]
+        x_codes.append(sb.tile([P, S], U32, name="x_codes1", tag="chain", align_bytes=64))
         for h in range(2):
             product(ym[h], w1_q[0], 0, h)
         per_half = HALF // 16
@@ -164,7 +177,10 @@ def tile_picked_yvitph_best_p_kernel(
             )
             product(ym[h], w1_q[1], 1, h)
 
-        w2_woven = [weave(w2_raw[o][:], f"w2_woven{o}") for o in range(PASSES)]
+        w2_woven = [sb.tile([P, N, PACK], BF16, name=f"w2_woven{o}", align_bytes=64) for o in range(PASSES)]
+        for o in range(PASSES):
+            weave(w2_woven[o][:], w2_raw[o])
+        w2_plane = [sb.tile([P, N], U8, name=f"w2_plane{o}", align_bytes=64) for o in range(PASSES)]
         halves = [(h, h * HALF, (h + 1) * HALF) for h in range(2)]
         delb = sb.tile([P, S], F32, name="delb")
         best = sb.tile([P, S], F32, name="best")
@@ -172,14 +188,18 @@ def tile_picked_yvitph_best_p_kernel(
         result = sb.tile([P, S], F32, name="result")
         for h, lo, hi in halves:
             nc.vector.tensor_tensor(here(mnew_p, lo, hi), ym[h][:], into_match[:, lo:hi], ADD)
-        w2_q0 = quantize(w2_woven[0], "w2_0")
+        w2_codes0 = late.tile([P, N], U32, name="w2_codes0", align_bytes=64, offset=2 * w2_bytes)
+        w2_q0 = (w2_codes0[:], w2_plane[0][:])
+        quantize(*w2_q0, w2_woven[0][:].rearrange("p m j -> p (m j)"))
         for h in range(2):
             product(yi[h], w2_q0, 0, h)
         for h, lo, hi in halves:
             nc.vector.tensor_tensor(
                 by4(here(dela_p, lo, hi)), row(gop_ps, lo, hi), by4(before(mnew_p, lo, hi)), ADD
             )
-        w2_q1 = quantize(w2_woven[1], "w2_1")
+        w2_codes1 = sb.tile([P, N], U32, name="w2_codes1", tag="into_match", align_bytes=64)
+        w2_q1 = (w2_codes1[:], w2_plane[1][:])
+        quantize(*w2_q1, w2_woven[1][:].rearrange("p m j -> p (m j)"))
         for h in range(2):
             product(yi[h], w2_q1, 1, h)
         for h, lo, hi in halves:

@@ -9,6 +9,7 @@ PACK = 4
 K_PASS = P * PACK
 PASSES = K // K_PASS
 HALF = S // 2
+BLOCKS = S // P
 PAD = 8
 QUADS = 4
 QUAD = P // QUADS
@@ -94,7 +95,7 @@ def tile_picked_yvitph_best_p_kernel(
         nc.vector.memset(mat_t[:, :PAD], 0.0)
         nc.vector.memset(x_planes[:].rearrange("p o s -> p (o s)").bitcast(I32), 0)
 
-        tmm_ps = ps.tile([P, PACK, P], F32, name="tmm_ps")
+        tmm_ps = ps.tile([P, PACK, P], F32, name="tmm_ps", tag="bank_t")
         gop_ps = ps.tile([P, PACK, P], F32, name="gop_ps")
         for cols, bank in ((gop_cols, gop_ps), (tmm_cols, tmm_ps)):
             for c in range(PACK):
@@ -120,8 +121,10 @@ def tile_picked_yvitph_best_p_kernel(
         s2 = sb.tile([P, S], F32, name="s2", tag="s2", align_bytes=64)
         s3 = sb.tile([P, S], F32, name="s3")
         s4 = sb.tile([P, S], F32, name="s4", tag="s4", align_bytes=64)
-        into_match = sb.tile([P, S], F32, name="into_match", tag="into_match", align_bytes=64)
-        into_insert = sb.tile([P, S], F32, name="into_insert")
+        into_match = [
+            sb.tile([P, HALF], F32, name=f"into_match{h}", tag=f"into_match{h}", align_bytes=64) for h in range(2)
+        ]
+        into_insert = sb.tile([P, S], F32, name="into_insert", tag="into_insert", align_bytes=64)
         nc.vector.tensor_tensor(by4(s1[:]), row(tmm_ps), by4(before(mat_p)), ADD)
         half_gop = sb.tile([P, S], F32, name="half_gop")
         ext_tmm = sb.tile([P, S], F32, name="ext_tmm")
@@ -132,7 +135,9 @@ def tile_picked_yvitph_best_p_kernel(
         nc.vector.tensor_tensor(by4(s3[:]), row(gop_ps), by4(here(mat_p)), ADD)
         x_codes = [sb.tile([P, S], U32, name="x_codes0", tag="mat", align_bytes=64)]
         nc.vector.tensor_copy(x_codes[0][:], word_table[0][:].indirect(offsets[:]))
-        nc.vector.tensor_tensor(into_match[:], s1[:], s2[:], MAX)
+        for h in range(2):
+            cols = slice(h * HALF, (h + 1) * HALF)
+            nc.vector.tensor_tensor(into_match[h][:], s1[:, cols], s2[:, cols], MAX)
         nc.vector.tensor_tensor(into_insert[:], s3[:], s4[:], MAX)
 
         def weave(woven, raw):
@@ -156,8 +161,28 @@ def tile_picked_yvitph_best_p_kernel(
                 stop=(o == PASSES - 1),
             )
 
-        ym = [ps.tile([P, HALF], F32, name=f"ym{h}") for h in range(2)]
-        yi = [ps.tile([P, HALF], F32, name=f"yi{h}") for h in range(2)]
+        def turned_product(weights, o):
+            codes, plane = weights
+            for b in range(BLOCKS):
+                cols = slice(b * P, (b + 1) * P)
+                nc.tensor.matmul_mx(
+                    out=yi_t[b][:],
+                    lhsT=x_codes[o][:, cols].bitcast(FP8X4),
+                    lhsT_scale=x_planes[:, o, cols],
+                    rhs=codes.bitcast(FP8X4),
+                    rhs_scale=plane,
+                    start=(o == 0),
+                    stop=(o == PASSES - 1),
+                )
+
+        ym = [ps.tile([P, HALF], F32, name=f"ym{h}", tag=f"bank_m{h}") for h in range(2)]
+        yi_t = [ps.tile([P, N], F32, name=f"yi_t{b}") for b in range(BLOCKS)]
+
+        insert_t_ps = ps.tile([P, BLOCKS, N], F32, name="insert_t_ps", tag="bank_t")
+        for b in range(BLOCKS):
+            nc.tensor.transpose(insert_t_ps[:, b, :], into_insert[:, b * P : (b + 1) * P], ident[:])
+        insert_t = sb.tile([P, BLOCKS, N], F32, name="insert_t")
+        nc.scalar.copy(insert_t[:], insert_t_ps[:])
 
         w1_woven = sb.tile([P, PASSES, N, PACK], BF16, name="w1_woven", tag="chain", align_bytes=64)
         for o in range(PASSES):
@@ -177,31 +202,47 @@ def tile_picked_yvitph_best_p_kernel(
             )
             product(ym[h], w1_q[1], 1, h)
 
-        w2_woven = [sb.tile([P, N, PACK], BF16, name=f"w2_woven{o}", align_bytes=64) for o in range(PASSES)]
+        w2_both_woven = sb.tile([P, PASSES, N, PACK], BF16, name="w2_woven", align_bytes=64)
+        w2_woven = [w2_both_woven[:, o] for o in range(PASSES)]
         for o in range(PASSES):
-            weave(w2_woven[o][:], w2_raw[o])
+            weave(w2_woven[o], w2_raw[o])
         w2_plane = [sb.tile([P, N], U8, name=f"w2_plane{o}", align_bytes=64) for o in range(PASSES)]
         halves = [(h, h * HALF, (h + 1) * HALF) for h in range(2)]
         delb = sb.tile([P, S], F32, name="delb")
         best = sb.tile([P, S], F32, name="best")
-        inew = sb.tile([P, S], F32, name="inew")
         result = sb.tile([P, S], F32, name="result")
         for h, lo, hi in halves:
-            nc.vector.tensor_tensor(here(mnew_p, lo, hi), ym[h][:], into_match[:, lo:hi], ADD)
+            nc.vector.tensor_tensor(here(mnew_p, lo, hi), ym[h][:], into_match[h][:], ADD)
         w2_codes0 = late.tile([P, N], U32, name="w2_codes0", align_bytes=64, offset=2 * w2_bytes)
         w2_q0 = (w2_codes0[:], w2_plane[0][:])
-        quantize(*w2_q0, w2_woven[0][:].rearrange("p m j -> p (m j)"))
-        for h in range(2):
-            product(yi[h], w2_q0, 0, h)
+        quantize(*w2_q0, w2_woven[0].rearrange("p m j -> p (m j)"))
+        turned_product(w2_q0, 0)
+        w2_codes1 = sb.tile([P, N], U32, name="w2_codes1", tag="into_match0", align_bytes=64)
+        w2_q1 = (w2_codes1[:], w2_plane[1][:])
+        quantize(*w2_q1, w2_woven[1].rearrange("p m j -> p (m j)"))
+        turned_product(w2_q1, 1)
+        half_yi_t = sb.tile([P, BLOCKS, N], F32, name="half_yi_t")
+        for b in range(BLOCKS):
+            nc.scalar.activation(half_yi_t[:, b, :], yi_t[b][:], COPY, scale=0.5)
+        inew = [
+            ps.tile([P, HALF], F32, name="inew0", tag="bank_t"),
+            ps.tile([P, HALF], F32, name="inew1", tag="bank_m0"),
+        ]
+        for term in (insert_t, half_yi_t):
+            for b in range(BLOCKS):
+                h, first = divmod(b * P, HALF)
+                nc.tensor.matmul(
+                    inew[h][:, first : first + P],
+                    term[:, b, :],
+                    ident[:],
+                    is_transpose=True,
+                    start=(term is insert_t and first == 0),
+                    stop=(term is half_yi_t and first + P == HALF),
+                )
         for h, lo, hi in halves:
             nc.vector.tensor_tensor(
                 by4(here(dela_p, lo, hi)), row(gop_ps, lo, hi), by4(before(mnew_p, lo, hi)), ADD
             )
-        w2_codes1 = sb.tile([P, N], U32, name="w2_codes1", tag="into_match", align_bytes=64)
-        w2_q1 = (w2_codes1[:], w2_plane[1][:])
-        quantize(*w2_q1, w2_woven[1][:].rearrange("p m j -> p (m j)"))
-        for h in range(2):
-            product(yi[h], w2_q1, 1, h)
         for h, lo, hi in halves:
             nc.vector.scalar_tensor_tensor(
                 delb[:, lo:hi], before(dela_p, lo, hi), -0.4, here(dela_p, lo, hi), ADD, MAX
@@ -209,8 +250,6 @@ def tile_picked_yvitph_best_p_kernel(
         for h, lo, hi in halves:
             nc.vector.tensor_tensor(best[:, lo:hi], here(mnew_p, lo, hi), delb[:, lo:hi], MAX)
         for h, lo, hi in halves:
-            nc.vector.scalar_tensor_tensor(inew[:, lo:hi], yi[h][:], 0.5, into_insert[:, lo:hi], MULT, ADD)
-        for h, lo, hi in halves:
-            nc.vector.tensor_tensor(result[:, lo:hi], best[:, lo:hi], inew[:, lo:hi], MAX)
-            queue = nc.sync if h == 0 else nc.scalar
+            nc.vector.tensor_tensor(result[:, lo:hi], inew[h][:], best[:, lo:hi], MAX)
+            queue = nc.scalar if h == 0 else nc.sync
             queue.dma_start(out[:, lo:hi], result[:, lo:hi])

@@ -42,19 +42,17 @@ def tile_picked_yvitph_best_p_kernel(
         w2_bytes = PASSES * PACK * N * 4
         scale_table = late.tile([P, T], U8, name="scale_table", align_bytes=64, offset=w2_bytes - 64)
         word_table = [
-            sb.tile([P, T], U32, name="word_table0", align_bytes=64),
+            sb.tile([P, T], U32, name="word_table0", tag="into_match1", align_bytes=64),
             late.tile([P, T], U32, name="word_table1", align_bytes=64, offset=w2_bytes),
         ]
         picked_rows = sb.tile([P, S], U8, name="picked_rows", align_bytes=64)
         x_planes = sb.tile([P, PASSES, S], U8, name="x_planes", align_bytes=64)
         tmm_cols = sb.tile([P, PACK], F32, name="tmm_cols")
         gop_cols = sb.tile([P, PACK], F32, name="gop_cols")
-        ext_col = sb.tile([P, 1], F32, name="ext_col", tag="chain", align_bytes=64)
+        ext_col = sb.tile([P, 1], F32, name="ext_col")
         ident = sb.tile([P, P], F32, name="ident")
-        mat_t = sb.tile([P, PAD + S], F32, name="mat_t", tag="mat", align_bytes=64)
-        mat_p = mat_t[:]
-        padded = sb.tile([P, 3, PAD + S], F32, name="padded")
-        ins_p, mnew_p, dela_p = (padded[:, i, :] for i in range(3))
+        padded = sb.tile([P, 4, PAD + S], F32, name="padded")
+        mat_p, ins_p, mnew_p, dela_p = (padded[:, i, :] for i in range(4))
 
         def here(t, lo=0, hi=S):
             return t[:, PAD + lo : PAD + hi]
@@ -75,8 +73,8 @@ def tile_picked_yvitph_best_p_kernel(
         nc.sync.dma_start(
             scale_table[top:, :].bitcast(I32), x_scales.rearrange("o r c -> r o c").bitcast(I32)
         )
-        nc.scalar.dma_start(gop_cols[:], gop[0].rearrange("(n c) -> n c", c=PACK))
         nc.scalar.dma_start(tmm_cols[:], tmm[0].rearrange("(n c) -> n c", c=PACK))
+        nc.scalar.dma_start(gop_cols[:], gop[0].rearrange("(n c) -> n c", c=PACK))
         nc.scalar.dma_start(ext_col[:], ext)
         nc.sync.dma_start(here(mat_p), mat)
         nc.sync.dma_start(here(ins_p), ins)
@@ -91,13 +89,14 @@ def tile_picked_yvitph_best_p_kernel(
 
         nc.vector.memset(scale_table[:top, :].bitcast(I32), 0)
         make_identity(nc, ident[:])
+        half = sb.tile([P, 1], F32, name="half", tag="chain", align_bytes=64)
+        nc.vector.memset(half[:], 0.5)
         nc.vector.memset(padded[:, :, :PAD], 0.0)
-        nc.vector.memset(mat_t[:, :PAD], 0.0)
         nc.vector.memset(x_planes[:].rearrange("p o s -> p (o s)").bitcast(I32), 0)
 
         tmm_ps = ps.tile([P, PACK, P], F32, name="tmm_ps", tag="bank_t")
         gop_ps = ps.tile([P, PACK, P], F32, name="gop_ps")
-        for cols, bank in ((gop_cols, gop_ps), (tmm_cols, tmm_ps)):
+        for cols, bank in ((tmm_cols, tmm_ps), (gop_cols, gop_ps)):
             for c in range(PACK):
                 nc.tensor.transpose(bank[:, c, :], cols[:, c : c + 1].to_broadcast([P, P]), ident[:])
 
@@ -117,28 +116,28 @@ def tile_picked_yvitph_best_p_kernel(
                 w2_raw[o], w2[o * K_PASS : (o + 1) * K_PASS, :].rearrange("(p j) m -> p j m", j=PACK)
             )
 
-        s1 = sb.tile([P, S], F32, name="s1")
+        s1 = sb.tile([P, S], F32, name="s1", tag="s1", align_bytes=64)
         s2 = sb.tile([P, S], F32, name="s2", tag="s2", align_bytes=64)
-        s3 = sb.tile([P, S], F32, name="s3")
+        s3 = sb.tile([P, S], F32, name="s3", tag="into_match0", align_bytes=64)
         s4 = sb.tile([P, S], F32, name="s4", tag="s4", align_bytes=64)
         into_match = [
             sb.tile([P, HALF], F32, name=f"into_match{h}", tag=f"into_match{h}", align_bytes=64) for h in range(2)
         ]
         into_insert = sb.tile([P, S], F32, name="into_insert", tag="into_insert", align_bytes=64)
-        nc.vector.tensor_tensor(by4(s1[:]), row(tmm_ps), by4(before(mat_p)), ADD)
         half_gop = sb.tile([P, S], F32, name="half_gop")
-        ext_tmm = sb.tile([P, S], F32, name="ext_tmm")
-        nc.scalar.activation(by4(half_gop[:]), row(gop_ps), COPY, scale=0.5)
-        nc.scalar.activation(by4(ext_tmm[:]), row(tmm_ps), COPY, scale=ext_col[:])
+        tmm_row = sb.tile([P, S], F32, name="tmm_row")
+        nc.scalar.copy(by4(tmm_row[:]), row(tmm_ps))
+        nc.scalar.activation(by4(half_gop[:]), row(gop_ps), COPY, scale=half[:])
+        nc.gpsimd.tensor_tensor(s1[:], before(mat_p), tmm_row[:], ADD)
         nc.gpsimd.tensor_tensor(s2[:], before(ins_p), half_gop[:], ADD)
-        nc.gpsimd.tensor_tensor(s4[:], here(ins_p), ext_tmm[:], ADD)
+        nc.vector.scalar_tensor_tensor(by4(s4[:]), row(tmm_ps), ext_col[:], by4(here(ins_p)), MULT, ADD)
         nc.vector.tensor_tensor(by4(s3[:]), row(gop_ps), by4(here(mat_p)), ADD)
-        x_codes = [sb.tile([P, S], U32, name="x_codes0", tag="mat", align_bytes=64)]
+        nc.vector.tensor_tensor(into_insert[:], s3[:], s4[:], MAX)
+        x_codes = [sb.tile([P, S], U32, name="x_codes0", tag="s4", align_bytes=64)]
         nc.vector.tensor_copy(x_codes[0][:], word_table[0][:].indirect(offsets[:]))
         for h in range(2):
             cols = slice(h * HALF, (h + 1) * HALF)
             nc.vector.tensor_tensor(into_match[h][:], s1[:, cols], s2[:, cols], MAX)
-        nc.vector.tensor_tensor(into_insert[:], s3[:], s4[:], MAX)
 
         def weave(woven, raw):
             nc.scalar.copy(
@@ -187,8 +186,8 @@ def tile_picked_yvitph_best_p_kernel(
         w1_woven = sb.tile([P, PASSES, N, PACK], BF16, name="w1_woven", tag="chain", align_bytes=64)
         for o in range(PASSES):
             weave(w1_woven[:, o], w1_raw[:, o])
-        w1_codes = sb.tile([P, PASSES * N], U32, name="w1_codes", tag="s4", align_bytes=64)
-        w1_plane = sb.tile([P, PASSES * N], U8, name="w1_plane", tag="s2", align_bytes=64)
+        w1_codes = sb.tile([P, PASSES * N], U32, name="w1_codes", tag="s2", align_bytes=64)
+        w1_plane = sb.tile([P, PASSES * N], U8, name="w1_plane", tag="s1", align_bytes=64)
         quantize(w1_codes[:], w1_plane[:], w1_woven[:].rearrange("p o m j -> p (o m j)"))
         w1_q = [(w1_codes[:, o * N : (o + 1) * N], w1_plane[:, o * N : (o + 1) * N]) for o in range(PASSES)]
         x_codes.append(sb.tile([P, S], U32, name="x_codes1", tag="chain", align_bytes=64))
@@ -202,7 +201,7 @@ def tile_picked_yvitph_best_p_kernel(
             )
             product(ym[h], w1_q[1], 1, h)
 
-        w2_both_woven = sb.tile([P, PASSES, N, PACK], BF16, name="w2_woven", align_bytes=64)
+        w2_both_woven = sb.tile([P, PASSES, N, PACK], BF16, name="w2_woven", tag="into_insert", align_bytes=64)
         w2_woven = [w2_both_woven[:, o] for o in range(PASSES)]
         for o in range(PASSES):
             weave(w2_woven[o], w2_raw[o])

from contextlib import ExitStack

import concourse.mybir as mybir
from concourse.masks import make_identity

K, T, S, N = 1024, 2048, 512, 128
P = 128
PACK = 4
K_PASS = P * PACK
PASSES = K // K_PASS
HALF = S // 2
BLOCKS = S // P
PAD = 8
QUADS = 4
QUAD = P // QUADS
ROWS = 4
FLOPS = 2 * 2 * K * N * S

F32 = mybir.dt.float32
BF16 = mybir.dt.bfloat16
I32 = mybir.dt.int32
U32 = mybir.dt.uint32
U16 = mybir.dt.uint16
U8 = mybir.dt.uint8
FP8X4 = mybir.dt.float8_e4m3fn_x4
ADD = mybir.AluOpType.add
MULT = mybir.AluOpType.mult
MAX = mybir.AluOpType.max
COPY = mybir.ActivationFunctionType.Copy


def tile_picked_yvitph_best_p_kernel(
    tc, x_words, x_scales, w1, w2, mat, ins, tmm, gop, ext, offs, out
):
    nc = tc.nc
    with ExitStack() as ctx:
        sb = ctx.enter_context(tc.tile_pool(name="sb", bufs=1))
        ps = ctx.enter_context(tc.psum_pool(name="ps", bufs=1))

        offsets = sb.tile([P, S // 16], U16, name="offsets")
        late = ctx.enter_context(tc.tile_pool(name="late", bufs=1))
        w2_bytes = PASSES * PACK * N * 4
        scale_table = late.tile([P, T], U8, name="scale_table", align_bytes=64, offset=w2_bytes - 64)
        word_table = [
            sb.tile([P, T], U32, name="word_table0", tag="into_match1", align_bytes=64),
            late.tile([P, T], U32, name="word_table1", align_bytes=64, offset=w2_bytes),
        ]
        picked_rows = sb.tile([P, S], U8, name="picked_rows", align_bytes=64)
        x_planes = sb.tile([P, PASSES, S], U8, name="x_planes", align_bytes=64)
        tmm_cols = sb.tile([P, PACK], F32, name="tmm_cols")
        gop_cols = sb.tile([P, PACK], F32, name="gop_cols")
        ext_col = sb.tile([P, 1], F32, name="ext_col")
        ident = sb.tile([P, P], F32, name="ident")
        padded = sb.tile([P, 4, PAD + S], F32, name="padded")
        mat_p, ins_p, mnew_p, dela_p = (padded[:, i, :] for i in range(4))

        def here(t, lo=0, hi=S):
            return t[:, PAD + lo : PAD + hi]

        def before(t, lo=0, hi=S):
            return t[:, PAD - 1 + lo : PAD - 1 + hi]

        def by4(ap):
            return ap.rearrange("p (n c) -> p n c", c=PACK)

        w1_raw = sb.tile([P, PASSES, PACK, N], F32, name="w1_raw")
        w2_both = late.tile([P, PASSES, PACK, N], F32, name="w2_both", align_bytes=64, offset=0)
        w2_raw = [w2_both[:, o] for o in range(PASSES)]

        n_rows = PASSES * QUADS * ROWS
        top = P - n_rows
        nc.sync.dma_start(offsets[:], offs)
        nc.sync.dma_start(
            scale_table[top:, :].bitcast(I32), x_scales.rearrange("o r c -> r o c").bitcast(I32)
        )
        nc.scalar.dma_start(tmm_cols[:], tmm[0].rearrange("(n c) -> n c", c=PACK))
        nc.scalar.dma_start(gop_cols[:], gop[0].rearrange("(n c) -> n c", c=PACK))
        nc.scalar.dma_start(ext_col[:], ext)
        nc.sync.dma_start(here(mat_p), mat)
        nc.sync.dma_start(here(ins_p), ins)

        def load_words(o):
            nc.sync.dma_start(
                word_table[o][:].bitcast(I32), x_words[o].rearrange("p n t -> p (n t)").bitcast(I32)
            )

        load_words(0)
        nc.sync.dma_start(w1_raw[:], w1.rearrange("(o p j) m -> p o j m", o=PASSES, j=PACK))

        nc.vector.memset(scale_table[:top, :].bitcast(I32), 0)
        make_identity(nc, ident[:])
        half = sb.tile([P, 1], F32, name="half", tag="chain", align_bytes=64)
        nc.vector.memset(half[:], 0.5)
        nc.vector.memset(padded[:, :, :PAD], 0.0)
        nc.vector.memset(x_planes[:].rearrange("p o s -> p (o s)").bitcast(I32), 0)

        tmm_ps = ps.tile([P, PACK, P], F32, name="tmm_ps", tag="bank_t")
        gop_ps = ps.tile([P, PACK, P], F32, name="gop_ps")
        for cols, bank in ((tmm_cols, tmm_ps), (gop_cols, gop_ps)):
            for c in range(PACK):
                nc.tensor.transpose(bank[:, c, :], cols[:, c : c + 1].to_broadcast([P, P]), ident[:])

        def row(bank, lo=0, hi=S):
            return bank[:].rearrange("p c n -> p n c")[:, lo // PACK : hi // PACK, :]

        nc.vector.tensor_copy(picked_rows[:], scale_table[:].indirect(offsets[:]))
        per_quad = PASSES * ROWS
        for q in range(QUADS):
            nc.sync.dma_start(
                x_planes[QUAD * q : QUAD * q + ROWS].rearrange("p o s -> p (o s)").bitcast(I32),
                picked_rows[top + per_quad * q : top + per_quad * (q + 1), :].bitcast(I32),
            )
        load_words(1)
        for o in range(PASSES):
            nc.sync.dma_start(
                w2_raw[o], w2[o * K_PASS : (o + 1) * K_PASS, :].rearrange("(p j) m -> p j m", j=PACK)
            )

        s1 = sb.tile([P, S], F32, name="s1", tag="s1", align_bytes=64)
        s2 = sb.tile([P, S], F32, name="s2", tag="s2", align_bytes=64)
        s3 = sb.tile([P, S], F32, name="s3", tag="into_match0", align_bytes=64)
        s4 = sb.tile([P, S], F32, name="s4", tag="s4", align_bytes=64)
        into_match = [
            sb.tile([P, HALF], F32, name=f"into_match{h}", tag=f"into_match{h}", align_bytes=64) for h in range(2)
        ]
        into_insert = sb.tile([P, S], F32, name="into_insert", tag="into_insert", align_bytes=64)
        half_gop = sb.tile([P, S], F32, name="half_gop")
        tmm_row = sb.tile([P, S], F32, name="tmm_row")
        nc.scalar.copy(by4(tmm_row[:]), row(tmm_ps))
        nc.scalar.activation(by4(half_gop[:]), row(gop_ps), COPY, scale=half[:])
        nc.gpsimd.tensor_tensor(s1[:], before(mat_p), tmm_row[:], ADD)
        nc.gpsimd.tensor_tensor(s2[:], before(ins_p), half_gop[:], ADD)
        nc.vector.scalar_tensor_tensor(by4(s4[:]), row(tmm_ps), ext_col[:], by4(here(ins_p)), MULT, ADD)
        nc.vector.tensor_tensor(by4(s3[:]), row(gop_ps), by4(here(mat_p)), ADD)
        nc.vector.tensor_tensor(into_insert[:], s3[:], s4[:], MAX)
        x_codes = [sb.tile([P, S], U32, name="x_codes0", tag="s4", align_bytes=64)]
        nc.vector.tensor_copy(x_codes[0][:], word_table[0][:].indirect(offsets[:]))
        for h in range(2):
            cols = slice(h * HALF, (h + 1) * HALF)
            nc.vector.tensor_tensor(into_match[h][:], s1[:, cols], s2[:, cols], MAX)

        def weave(woven, raw):
            nc.scalar.copy(
                woven.rearrange("p (c i) j -> p c j i", i=4), raw.rearrange("p j (c i) -> p c j i", i=4)
            )

        def quantize(codes, plane, woven):
            nc.vector.quantize_mx(out=codes.bitcast(FP8X4), scales=plane, in_=woven)

        def product(bank, weights, o, h):
            codes, plane = weights
            cols = slice(h * HALF, (h + 1) * HALF)
            nc.tensor.matmul_mx(
                out=bank[:],
                lhsT=codes.bitcast(FP8X4),
                lhsT_scale=plane,
                rhs=x_codes[o][:, cols].bitcast(FP8X4),
                rhs_scale=x_planes[:, o, cols],
                start=(o == 0),
                stop=(o == PASSES - 1),
            )

        def turned_product(weights, o):
            codes, plane = weights
            for b in range(BLOCKS):
                cols = slice(b * P, (b + 1) * P)
                nc.tensor.matmul_mx(
                    out=yi_t[b][:],
                    lhsT=x_codes[o][:, cols].bitcast(FP8X4),
                    lhsT_scale=x_planes[:, o, cols],
                    rhs=codes.bitcast(FP8X4),
                    rhs_scale=plane,
                    start=(o == 0),
                    stop=(o == PASSES - 1),
                )

        ym = [ps.tile([P, HALF], F32, name=f"ym{h}", tag=f"bank_m{h}") for h in range(2)]
        yi_t = [ps.tile([P, N], F32, name=f"yi_t{b}") for b in range(BLOCKS)]

        insert_t_ps = ps.tile([P, BLOCKS, N], F32, name="insert_t_ps", tag="bank_t")
        for b in range(BLOCKS):
            nc.tensor.transpose(insert_t_ps[:, b, :], into_insert[:, b * P : (b + 1) * P], ident[:])
        insert_t = sb.tile([P, BLOCKS, N], F32, name="insert_t")
        nc.scalar.copy(insert_t[:], insert_t_ps[:])

        w1_woven = sb.tile([P, PASSES, N, PACK], BF16, name="w1_woven", tag="chain", align_bytes=64)
        for o in range(PASSES):
            weave(w1_woven[:, o], w1_raw[:, o])
        w1_codes = sb.tile([P, PASSES * N], U32, name="w1_codes", tag="s2", align_bytes=64)
        w1_plane = sb.tile([P, PASSES * N], U8, name="w1_plane", tag="s1", align_bytes=64)
        quantize(w1_codes[:], w1_plane[:], w1_woven[:].rearrange("p o m j -> p (o m j)"))
        w1_q = [(w1_codes[:, o * N : (o + 1) * N], w1_plane[:, o * N : (o + 1) * N]) for o in range(PASSES)]
        x_codes.append(sb.tile([P, S], U32, name="x_codes1", tag="chain", align_bytes=64))
        for h in range(2):
            product(ym[h], w1_q[0], 0, h)
        per_half = HALF // 16
        for h in range(2):
            nc.vector.tensor_copy(
                x_codes[1][:, h * HALF : (h + 1) * HALF],
                word_table[1][:].indirect(offsets[:, h * per_half : (h + 1) * per_half]),
            )
            product(ym[h], w1_q[1], 1, h)

        w2_both_woven = sb.tile([P, PASSES, N, PACK], BF16, name="w2_woven", tag="into_insert", align_bytes=64)
        w2_woven = [w2_both_woven[:, o] for o in range(PASSES)]
        for o in range(PASSES):
            weave(w2_woven[o], w2_raw[o])
        w2_plane = [sb.tile([P, N], U8, name=f"w2_plane{o}", align_bytes=64) for o in range(PASSES)]
        halves = [(h, h * HALF, (h + 1) * HALF) for h in range(2)]
        delb = sb.tile([P, S], F32, name="delb")
        best = sb.tile([P, S], F32, name="best")
        result = sb.tile([P, S], F32, name="result")
        for h, lo, hi in halves:
            nc.vector.tensor_tensor(here(mnew_p, lo, hi), ym[h][:], into_match[h][:], ADD)
        w2_codes0 = late.tile([P, N], U32, name="w2_codes0", align_bytes=64, offset=2 * w2_bytes)
        w2_q0 = (w2_codes0[:], w2_plane[0][:])
        quantize(*w2_q0, w2_woven[0].rearrange("p m j -> p (m j)"))
        turned_product(w2_q0, 0)
        w2_codes1 = sb.tile([P, N], U32, name="w2_codes1", tag="into_match0", align_bytes=64)
        w2_q1 = (w2_codes1[:], w2_plane[1][:])
        quantize(*w2_q1, w2_woven[1].rearrange("p m j -> p (m j)"))
        turned_product(w2_q1, 1)
        half_yi_t = sb.tile([P, BLOCKS, N], F32, name="half_yi_t")
        for b in range(BLOCKS):
            nc.scalar.activation(half_yi_t[:, b, :], yi_t[b][:], COPY, scale=0.5)
        inew = [
            ps.tile([P, HALF], F32, name="inew0", tag="bank_t"),
            ps.tile([P, HALF], F32, name="inew1", tag="bank_m0"),
        ]
        for term in (insert_t, half_yi_t):
            for b in range(BLOCKS):
                h, first = divmod(b * P, HALF)
                nc.tensor.matmul(
                    inew[h][:, first : first + P],
                    term[:, b, :],
                    ident[:],
                    is_transpose=True,
                    start=(term is insert_t and first == 0),
                    stop=(term is half_yi_t and first + P == HALF),
                )
        for h, lo, hi in halves:
            nc.vector.tensor_tensor(
                by4(here(dela_p, lo, hi)), row(gop_ps, lo, hi), by4(before(mnew_p, lo, hi)), ADD
            )
        for h, lo, hi in halves:
            nc.vector.scalar_tensor_tensor(
                delb[:, lo:hi], before(dela_p, lo, hi), -0.4, here(dela_p, lo, hi), ADD, MAX
            )
        for h, lo, hi in halves:
            nc.vector.tensor_tensor(best[:, lo:hi], here(mnew_p, lo, hi), delb[:, lo:hi], MAX)
        for h, lo, hi in halves:
            nc.vector.tensor_tensor(result[:, lo:hi], inew[h][:], best[:, lo:hi], MAX)
            queue = nc.scalar if h == 0 else nc.sync
            queue.dma_start(out[:, lo:hi], result[:, lo:hi])
